import numpy as np
import ml_dtypes


def mxq(x, axis, fmt="e4m3"):
    dtype, down = {"e4m3": (ml_dtypes.float8_e4m3fn, 7), "e5m2": (ml_dtypes.float8_e5m2, 14)}[fmt]
    v = np.moveaxis(np.asarray(x, np.float32).astype(ml_dtypes.bfloat16).astype(np.float64), axis, -1)
    blocks = v.reshape(v.shape[:-1] + (-1, 32))
    amax = np.abs(blocks).max(-1, keepdims=True)
    byte = np.maximum(np.where(amax > 0, np.frexp(amax)[1] - 1 + 127, 0) - down, 1)
    scale = np.exp2(byte - 127.0)
    codes = (blocks / scale).astype(np.float32).astype(dtype).astype(np.float64)
    return np.moveaxis((codes * scale).reshape(v.shape), -1, axis)


WIDE = False


def mx_kscale(k):
    if not WIDE:
        return np.ones(k)
    levels = np.array([30, -30])
    if k % 512:
        return np.exp2(np.random.permutation(np.resize(levels, k // 32))).repeat(32)
    a = np.empty((k // 512, 16))
    for p in range(k // 512):
        a[p, :8] = np.random.permutation(np.resize(levels, 8))
        for g in range(8):
            far = levels[np.abs(levels - a[p, g]) >= 10]
            a[p, g + 8] = far[np.random.randint(len(far))]
    return np.exp2(a.ravel()).repeat(32)


def f64(x):
    return np.asarray(x).astype(np.float64)


def striped(idx):
    return np.tile(np.asarray(idx).reshape(-1, 16).T, (8, 1)).astype(np.uint16)


def unstriped(offs):
    return offs[:16].T.reshape(-1).astype(np.int64)


def striped8(idx):
    return np.asarray(idx).reshape(8, -1, 16).transpose(0, 2, 1).reshape(128, -1).astype(np.uint16)


def unstriped8(offs):
    return offs.reshape(8, 16, -1).transpose(0, 2, 1).reshape(8, -1).astype(np.int64)


def pick8(x, idx, run):
    r = np.arange(len(x))
    return x[r[:, None], idx[r % (8 * run) // run]]


E2M1 = np.array([0.0, 0.5, 1.0, 1.5, 2.0, 3.0, 4.0, 6.0, -0.0, -0.5, -1.0, -1.5, -2.0, -3.0, -4.0, -6.0])


def pack_weight(w, fmt):
    k, n = w.shape
    w = f64(np.asarray(w, np.float32).astype(ml_dtypes.bfloat16)).reshape(k // 32, 32, n)
    amax = np.abs(w).max(1)
    if fmt == "e4m3":
        byte = np.frexp(amax)[1] - 1 + 127 - 7
    else:
        mant, ex = np.frexp(amax / 6.0)
        byte = np.where(mant > 0.5, ex, ex - 1) + 127
    byte = np.clip(np.where(amax > 0, byte, 1), 1, 254)
    scaled = (w * np.exp2(127.0 - byte)[:, None, :]).reshape(k, n).astype(np.float32)
    by_word = np.ascontiguousarray(scaled.reshape(k // 512, 128, 4, n).transpose(0, 1, 3, 2))
    if fmt == "e4m3":
        words = by_word.astype(ml_dtypes.float8_e4m3fn).view(np.uint8)
    else:
        c = by_word.astype(ml_dtypes.float4_e2m1fn).view(np.uint8) & 0xF
        words = (c[..., 0::2] | (c[..., 1::2] << 4)).reshape(k // 512, 128, 2 * n)
    return np.ascontiguousarray(words), np.ascontiguousarray(byte.astype(np.uint8).reshape(k // 512, 16, n))


def unpack_weight(words, scales, fmt):
    g, _, n = scales.shape
    words = np.ascontiguousarray(words).reshape(g, 128, n, -1)
    if fmt == "e4m3":
        vals = words.view(ml_dtypes.float8_e4m3fn).astype(np.float64)
    else:
        nib = np.empty((g, 128, n, 4), np.uint8)
        nib[..., 0::2] = words & 0xF
        nib[..., 1::2] = words >> 4
        vals = E2M1[nib]
    vals = vals * np.repeat(np.exp2(scales.astype(np.float64) - 127.0), 8, axis=1)[..., None]
    return vals.transpose(0, 1, 3, 2).reshape(g * 512, n)


N, K, T, J, V = 512, 512, 1024, 512, 1024


def setup_inputs():
    n = np.random.standard_normal
    idx = np.stack([np.random.permutation(T)[:J] for _ in range(8)])
    idx2 = np.random.permutation(V)[:J]
    fn = mx_kscale(N)
    wp = pack_weight(n((N, K)) * 1 / np.sqrt(N) * fn[:, None], "e2m1")
    return {
        "g": (n((N, T)) * np.exp(0.5 * n((1, T))) / fn[:, None]).astype(np.float32),
        "tb": (n((N, V))).astype(np.float32),
        "w_words": wp[0],
        "w_scales": wp[1],
        "rw": (np.random.uniform(0.5, 2.0, (1, J))).astype(np.float32),
        "offs": striped8(idx),
        "offs2": striped(idx2),
    }


def reference(g, tb, w_words, w_scales, rw, offs, offs2):
    idx = unstriped8(offs)
    idx2 = unstriped(offs2)
    wu = unpack_weight(w_words, w_scales, "e2m1")
    d = pick8(f64(g), idx, 64) * f64(tb)[:, idx2]
    dq = mxq(d, 0, "e5m2")
    p = wu.T @ dq
    y = p * f64(rw)
    return y

@@ -1,0 +1,104 @@
+from contextlib import ExitStack
+
+import concourse.mybir as mybir
+from concourse.masks import make_identity
+
+F32 = mybir.dt.float32
+BF16 = mybir.dt.bfloat16
+I32 = mybir.dt.int32
+U32 = mybir.dt.uint32
+U16 = mybir.dt.uint16
+U8 = mybir.dt.uint8
+E5M2X4 = mybir.dt.float8_e5m2_x4
+E2M1X4 = mybir.dt.float4_e2m1fn_x4
+MULT = mybir.AluOpType.mult
+
+N, K, T, J, V = 512, 512, 1024, 512, 1024
+P = 128
+PACK = 4
+HALF = J // 2
+FLOPS = 2 * N * K * J
+
+
+def tile_moe_expert_head_gradients_by_table_kernel(tc, g, tb, w_words, w_scales, rw, offs, offs2, out):
+    nc = tc.nc
+    with ExitStack() as ctx:
+        keep = ctx.enter_context(tc.tile_pool(name="keep", bufs=1))
+        psum = ctx.enter_context(tc.psum_pool(name="psum", bufs=1))
+
+        g_list = keep.tile([P, J // 16], U16, name="g_list")
+        tb_list = keep.tile([P, J // 16], U16, name="tb_list")
+        g_rows = g.rearrange("(p r) t -> r p t", r=PACK)
+        tb_rows = tb.rearrange("(p r) v -> r p v", r=PACK)
+        g_win = [keep.tile([P, T], F32, name=f"g_win{r}") for r in range(PACK)]
+        tb_win = [keep.tile([P, V], F32, name=f"tb_win{r}") for r in range(PACK)]
+        words = keep.tile([P, 2 * K], U8, name="words", align_bytes=64)
+        w_plane = keep.tile([P, K], U8, name="w_plane", align_bytes=64)
+        rw_cols = keep.tile([P, PACK], F32, name="rw_cols")
+        ident = keep.tile([P, P], F32, name="ident")
+        rw_all = keep.tile([P, J], F32, name="rw_all")
+
+        nc.vector.memset(w_plane[:].bitcast(I32), 0)
+        make_identity(nc, ident[:])
+
+        nc.sync.dma_start(tb_list[:], offs2)
+        nc.sync.dma_start(tb_win[0][:], tb_rows[0])
+        nc.sync.dma_start(g_list[:], offs)
+        nc.sync.dma_start(g_win[0][:], g_rows[0])
+        nc.scalar.dma_start(rw_cols[:], rw.rearrange("o (p c) -> (o p) c", c=PACK))
+        for r in range(1, PACK):
+            nc.sync.dma_start(tb_win[r][:], tb_rows[r])
+            nc.sync.dma_start(g_win[r][:], g_rows[r])
+        nc.sync.dma_start(words[:].bitcast(I32), w_words[0].bitcast(I32))
+        scale_rows = w_scales[0].bitcast(I32).rearrange("(q r) c -> r q c", r=4)
+        for r in range(4):
+            nc.sync.dma_start(w_plane[r:P:32, :].bitcast(I32), scale_rows[r])
+
+        rw_bank = psum.tile([P, PACK, P], F32, name="rw_bank")
+        for c in range(PACK):
+            nc.tensor.transpose(rw_bank[:, c, :], rw_cols[:, c : c + 1].to_broadcast([P, P]), ident[:])
+        nc.scalar.copy(rw_all[:].rearrange("p (n c) -> p n c", c=PACK), rw_bank[:].rearrange("p c n -> p n c"))
+
+        tb_got = [keep.tile([P, J], F32, name=f"tb_got{r}") for r in range(PACK)]
+        d_pair = [keep.tile([P, 2, J], F32, name=f"d_pair{u}") for u in range(2)]
+        grouped = [keep.tile([P, HALF, PACK], BF16, name=f"grouped{h}", align_bytes=64) for h in range(2)]
+        codes = keep.tile([P, J], U32, name="codes", align_bytes=64)
+        d_plane = keep.tile([P, J], U8, name="d_plane", align_bytes=64)
+
+        def weave(copy, u, h):
+            copy(grouped[h][:, :, 2 * u : 2 * u + 2], d_pair[u][:, :, h * HALF : (h + 1) * HALF].rearrange("p e j -> p j e"))
+
+        for r in range(PACK):
+            nc.vector.tensor_copy(tb_got[r][:], tb_win[r][:].indirect(tb_list[:]))
+            if r < PACK - 1:
+                nc.vector.tensor_tensor(d_pair[r // 2][:, r % 2, :], g_win[r][:].indirect(g_list[:]), tb_got[r][:], MULT)
+            if r == 1:
+                weave(nc.scalar.copy, 0, 0)
+                weave(nc.scalar.copy, 0, 1)
+        for h in range(2):
+            cols = slice(h * HALF, (h + 1) * HALF)
+            nc.vector.tensor_tensor(
+                d_pair[1][:, 1, cols], g_win[3][:].indirect(g_list[:, h * 16 : (h + 1) * 16]), tb_got[3][:, cols], MULT
+            )
+        weave(nc.scalar.copy, 1, 0)
+        weave(nc.vector.tensor_copy, 1, 1)
+        for h in range(2):
+            cols = slice(h * HALF, (h + 1) * HALF)
+            nc.vector.quantize_mx(
+                out=codes[:, cols].bitcast(E5M2X4), scales=d_plane[:, cols], in_=grouped[h][:].rearrange("p j r -> p (j r)")
+            )
+
+        for m in range(K // P):
+            acc = psum.tile([P, J], F32, name=f"acc{m}")
+            nc.tensor.matmul_mx(
+                out=acc[:],
+                lhsT=words[:, 2 * P * m : 2 * P * (m + 1)].bitcast(E2M1X4),
+                lhsT_scale=w_plane[:, P * m : P * (m + 1)],
+                rhs=codes[:].bitcast(E5M2X4),
+                rhs_scale=d_plane[:],
+                start=True,
+                stop=True,
+            )
+            res = keep.tile([P, J], F32, name=f"res{m}")
+            nc.vector.tensor_tensor(res[:], acc[:], rw_all[:], MULT)
+            nc.sync.dma_start(out[P * m : P * (m + 1), :], res[:])

@@ -41,14 +41,16 @@ def tile_moe_expert_head_gradients_by_table_kernel(tc, g, tb, w_words, w_scales,
         nc.vector.memset(w_plane[:].bitcast(I32), 0)
         make_identity(nc, ident[:])
 
-        nc.sync.dma_start(tb_list[:], offs2)
         nc.sync.dma_start(tb_win[0][:], tb_rows[0])
+        nc.sync.dma_start(tb_list[:], offs2)
+        nc.sync.dma_start(tb_win[1][:], tb_rows[1])
         nc.sync.dma_start(g_list[:], offs)
-        nc.sync.dma_start(g_win[0][:], g_rows[0])
-        nc.scalar.dma_start(rw_cols[:], rw.rearrange("o (p c) -> (o p) c", c=PACK))
-        for r in range(1, PACK):
-            nc.sync.dma_start(tb_win[r][:], tb_rows[r])
+        for r in range(PACK):
             nc.sync.dma_start(g_win[r][:], g_rows[r])
+            if r == 0:
+                nc.sync.dma_start(rw_cols[:], rw.rearrange("o (p c) -> (o p) c", c=PACK))
+            if r + 2 < PACK:
+                nc.sync.dma_start(tb_win[r + 2][:], tb_rows[r + 2])
         nc.sync.dma_start(words[:].bitcast(I32), w_words[0].bitcast(I32))
         scale_rows = w_scales[0].bitcast(I32).rearrange("(q r) c -> r q c", r=4)
         for r in range(4):
@@ -65,23 +67,34 @@ def tile_moe_expert_head_gradients_by_table_kernel(tc, g, tb, w_words, w_scales,
         codes = keep.tile([P, J], U32, name="codes", align_bytes=64)
         d_plane = keep.tile([P, J], U8, name="d_plane", align_bytes=64)
 
-        def weave(copy, u, h):
-            copy(grouped[h][:, :, 2 * u : 2 * u + 2], d_pair[u][:, :, h * HALF : (h + 1) * HALF].rearrange("p e j -> p j e"))
-
-        for r in range(PACK):
-            nc.vector.tensor_copy(tb_got[r][:], tb_win[r][:].indirect(tb_list[:]))
-            if r < PACK - 1:
-                nc.vector.tensor_tensor(d_pair[r // 2][:, r % 2, :], g_win[r][:].indirect(g_list[:]), tb_got[r][:], MULT)
-            if r == 1:
-                weave(nc.scalar.copy, 0, 0)
-                weave(nc.scalar.copy, 0, 1)
-        for h in range(2):
-            cols = slice(h * HALF, (h + 1) * HALF)
-            nc.vector.tensor_tensor(
-                d_pair[1][:, 1, cols], g_win[3][:].indirect(g_list[:, h * 16 : (h + 1) * 16]), tb_got[3][:, cols], MULT
+        def weave(copy, u, j0, j1):
+            h = j0 // HALF
+            copy(
+                grouped[h][:, j0 - h * HALF : j1 - h * HALF, 2 * u : 2 * u + 2],
+                d_pair[u][:, :, j0:j1].rearrange("p e j -> p j e"),
             )
-        weave(nc.scalar.copy, 1, 0)
-        weave(nc.vector.tensor_copy, 1, 1)
+
+        def gather_tb(r):
+            nc.vector.tensor_copy(tb_got[r][:], tb_win[r][:].indirect(tb_list[:]))
+
+        def gather_g(r, j0, j1):
+            nc.vector.tensor_tensor(
+                d_pair[r // 2][:, r % 2, j0:j1], g_win[r][:].indirect(g_list[:, j0 // 16 : j1 // 16]), tb_got[r][:, j0:j1], MULT
+            )
+
+        gather_tb(0)
+        for r in range(PACK - 1):
+            gather_tb(r + 1)
+            gather_g(r, 0, J)
+            if r == 1:
+                weave(nc.scalar.copy, 0, 0, HALF)
+                weave(nc.scalar.copy, 0, HALF, J)
+        pieces = [(0, 256), (256, 384), (384, 512)]
+        for j0, j1 in pieces:
+            gather_g(PACK - 1, j0, j1)
+        weave(nc.scalar.copy, 1, *pieces[0])
+        for j0, j1 in pieces[1:]:
+            weave(nc.vector.tensor_copy, 1, j0, j1)
         for h in range(2):
             cols = slice(h * HALF, (h + 1) * HALF)
             nc.vector.quantize_mx(
@@ -100,5 +113,7 @@ def tile_moe_expert_head_gradients_by_table_kernel(tc, g, tb, w_words, w_scales,
                 stop=True,
             )
             res = keep.tile([P, J], F32, name=f"res{m}")
-            nc.vector.tensor_tensor(res[:], acc[:], rw_all[:], MULT)
-            nc.sync.dma_start(out[P * m : P * (m + 1), :], res[:])
+            cuts = [slice(0, HALF), slice(HALF, J)] if m in (0, K // P - 1) else [slice(0, J)]
+            for cols in cuts:
+                nc.vector.tensor_tensor(res[:, cols], acc[:, cols], rw_all[:, cols], MULT)
+                nc.sync.dma_start(out[P * m : P * (m + 1), cols], res[:, cols])

from contextlib import ExitStack

import concourse.mybir as mybir
from concourse.masks import make_identity

F32 = mybir.dt.float32
BF16 = mybir.dt.bfloat16
I32 = mybir.dt.int32
U32 = mybir.dt.uint32
U16 = mybir.dt.uint16
U8 = mybir.dt.uint8
E5M2X4 = mybir.dt.float8_e5m2_x4
E2M1X4 = mybir.dt.float4_e2m1fn_x4
MULT = mybir.AluOpType.mult

N, K, T, J, V = 512, 512, 1024, 512, 1024
P = 128
PACK = 4
HALF = J // 2
FLOPS = 2 * N * K * J


def tile_moe_expert_head_gradients_by_table_kernel(tc, g, tb, w_words, w_scales, rw, offs, offs2, out):
    nc = tc.nc
    with ExitStack() as ctx:
        keep = ctx.enter_context(tc.tile_pool(name="keep", bufs=1))
        psum = ctx.enter_context(tc.psum_pool(name="psum", bufs=1))

        g_list = keep.tile([P, J // 16], U16, name="g_list")
        tb_list = keep.tile([P, J // 16], U16, name="tb_list")
        g_rows = g.rearrange("(p r) t -> r p t", r=PACK)
        tb_rows = tb.rearrange("(p r) v -> r p v", r=PACK)
        g_win = [keep.tile([P, T], F32, name=f"g_win{r}") for r in range(PACK)]
        tb_win = [keep.tile([P, V], F32, name=f"tb_win{r}") for r in range(PACK)]
        words = keep.tile([P, 2 * K], U8, name="words", align_bytes=64)
        w_plane = keep.tile([P, K], U8, name="w_plane", align_bytes=64)
        rw_cols = keep.tile([P, PACK], F32, name="rw_cols")
        ident = keep.tile([P, P], F32, name="ident")
        rw_all = keep.tile([P, J], F32, name="rw_all")

        nc.vector.memset(w_plane[:].bitcast(I32), 0)
        make_identity(nc, ident[:])

        nc.sync.dma_start(tb_win[0][:], tb_rows[0])
        nc.sync.dma_start(tb_list[:], offs2)
        nc.sync.dma_start(tb_win[1][:], tb_rows[1])
        nc.sync.dma_start(g_list[:], offs)
        for r in range(PACK):
            nc.sync.dma_start(g_win[r][:], g_rows[r])
            if r == 0:
                nc.sync.dma_start(rw_cols[:], rw.rearrange("o (p c) -> (o p) c", c=PACK))
            if r + 2 < PACK:
                nc.sync.dma_start(tb_win[r + 2][:], tb_rows[r + 2])
        nc.sync.dma_start(words[:].bitcast(I32), w_words[0].bitcast(I32))
        scale_rows = w_scales[0].bitcast(I32).rearrange("(q r) c -> r q c", r=4)
        for r in range(4):
            nc.sync.dma_start(w_plane[r:P:32, :].bitcast(I32), scale_rows[r])

        rw_bank = psum.tile([P, PACK, P], F32, name="rw_bank")
        for c in range(PACK):
            nc.tensor.transpose(rw_bank[:, c, :], rw_cols[:, c : c + 1].to_broadcast([P, P]), ident[:])
        nc.scalar.copy(rw_all[:].rearrange("p (n c) -> p n c", c=PACK), rw_bank[:].rearrange("p c n -> p n c"))

        tb_got = [keep.tile([P, J], F32, name=f"tb_got{r}") for r in range(PACK)]
        d_pair = [keep.tile([P, 2, J], F32, name=f"d_pair{u}") for u in range(2)]
        grouped = [keep.tile([P, HALF, PACK], BF16, name=f"grouped{h}", align_bytes=64) for h in range(2)]
        codes = keep.tile([P, J], U32, name="codes", align_bytes=64)
        d_plane = keep.tile([P, J], U8, name="d_plane", align_bytes=64)

        def weave(copy, u, j0, j1):
            h = j0 // HALF
            copy(
                grouped[h][:, j0 - h * HALF : j1 - h * HALF, 2 * u : 2 * u + 2],
                d_pair[u][:, :, j0:j1].rearrange("p e j -> p j e"),
            )

        def gather_tb(r):
            nc.vector.tensor_copy(tb_got[r][:], tb_win[r][:].indirect(tb_list[:]))

        def gather_g(r, j0, j1):
            nc.vector.tensor_tensor(
                d_pair[r // 2][:, r % 2, j0:j1], g_win[r][:].indirect(g_list[:, j0 // 16 : j1 // 16]), tb_got[r][:, j0:j1], MULT
            )

        gather_tb(0)
        for r in range(PACK - 1):
            gather_tb(r + 1)
            gather_g(r, 0, J)
            if r == 1:
                weave(nc.scalar.copy, 0, 0, HALF)
                weave(nc.scalar.copy, 0, HALF, J)
        pieces = [(0, 256), (256, 384), (384, 512)]
        for j0, j1 in pieces:
            gather_g(PACK - 1, j0, j1)
        weave(nc.scalar.copy, 1, *pieces[0])
        for j0, j1 in pieces[1:]:
            weave(nc.vector.tensor_copy, 1, j0, j1)
        for h in range(2):
            cols = slice(h * HALF, (h + 1) * HALF)
            nc.vector.quantize_mx(
                out=codes[:, cols].bitcast(E5M2X4), scales=d_plane[:, cols], in_=grouped[h][:].rearrange("p j r -> p (j r)")
            )

        for m in range(K // P):
            acc = psum.tile([P, J], F32, name=f"acc{m}")
            nc.tensor.matmul_mx(
                out=acc[:],
                lhsT=words[:, 2 * P * m : 2 * P * (m + 1)].bitcast(E2M1X4),
                lhsT_scale=w_plane[:, P * m : P * (m + 1)],
                rhs=codes[:].bitcast(E5M2X4),
                rhs_scale=d_plane[:],
                start=True,
                stop=True,
            )
            res = keep.tile([P, J], F32, name=f"res{m}")
            cuts = [slice(0, HALF), slice(HALF, J)] if m in (0, K // P - 1) else [slice(0, J)]
            for cols in cuts:
                nc.vector.tensor_tensor(res[:, cols], acc[:, cols], rw_all[:, cols], MULT)
                nc.sync.dma_start(out[P * m : P * (m + 1), cols], res[:, cols])
